import numpy as np
import ml_dtypes


def mxq(x, axis, fmt="e4m3"):
    dtype, down = {"e4m3": (ml_dtypes.float8_e4m3fn, 7), "e5m2": (ml_dtypes.float8_e5m2, 14)}[fmt]
    v = np.moveaxis(np.asarray(x, np.float32).astype(ml_dtypes.bfloat16).astype(np.float64), axis, -1)
    blocks = v.reshape(v.shape[:-1] + (-1, 32))
    amax = np.abs(blocks).max(-1, keepdims=True)
    byte = np.maximum(np.where(amax > 0, np.frexp(amax)[1] - 1 + 127, 0) - down, 1)
    scale = np.exp2(byte - 127.0)
    codes = (blocks / scale).astype(np.float32).astype(dtype).astype(np.float64)
    return np.moveaxis((codes * scale).reshape(v.shape), -1, axis)


WIDE = False


def mx_kscale(k):
    if not WIDE:
        return np.ones(k)
    levels = np.array([10, -10, 5, -5, 0])
    if k % 512:
        return np.exp2(np.random.permutation(np.resize(levels, k // 32))).repeat(32)
    a = np.empty((k // 512, 16))
    for p in range(k // 512):
        a[p, :8] = np.random.permutation(np.resize(levels, 8))
        for g in range(8):
            far = levels[np.abs(levels - a[p, g]) >= 10]
            a[p, g + 8] = far[np.random.randint(len(far))]
    return np.exp2(a.ravel()).repeat(32)


def f64(x):
    return np.asarray(x).astype(np.float64)


def striped(idx):
    return np.tile(idx.reshape(-1, 16).T, (8, 1)).astype(np.uint16)


def unstriped(offs):
    return offs[:16].T.reshape(-1).astype(np.int64)


def striped8(idx):
    return np.concatenate([x.reshape(-1, 16).T for x in idx]).astype(np.uint16)


def runs(offs, k):
    lists = np.stack([offs[16 * r : 16 * r + 16].T.reshape(-1) for r in range(8)]).astype(np.int64)
    return lists[np.arange(k) % 512 // 64]


def pack_weight(w):
    k, n = w.shape
    w = f64(np.asarray(w, np.float32).astype(ml_dtypes.bfloat16)).reshape(k // 32, 32, n)
    amax = np.abs(w).max(1)
    byte = np.clip(np.where(amax > 0, np.frexp(amax)[1] - 1 + 127 - 7, 1), 1, 254)
    scaled = (w * np.exp2(127.0 - byte)[:, None, :]).reshape(k, n).astype(np.float32)
    words = np.ascontiguousarray(scaled.reshape(k // 512, 128, 4, n).transpose(0, 1, 3, 2)).astype(ml_dtypes.float8_e4m3fn).view(np.uint8)
    return words, np.ascontiguousarray(byte.astype(np.uint8).reshape(k // 512, 16, n))


def unpack_weight(words, scales):
    g, p, n, _ = words.shape
    vals = np.ascontiguousarray(words).view(ml_dtypes.float8_e4m3fn).astype(np.float64) * np.repeat(np.exp2(scales.astype(np.float64) - 127.0), 8, axis=1)[..., None]
    return vals.transpose(0, 1, 3, 2).reshape(g * 512, n)


K, T, S, H, C = 512, 2048, 512, 512, 512


def setup_inputs():
    n = np.random.standard_normal
    s = mx_kscale(K)[:, None]
    packed_xT = pack_weight(n((K, T)) * s)
    return {
        "x_words": packed_xT[0],
        "x_scales": packed_xT[1],
        "w1": (n((K, H)) / np.sqrt(K) / s).astype(np.float32),
        "tau": np.random.uniform(0.3, 0.9, (H, 1)).astype(np.float32),
        "gs": (np.random.uniform(0.5, 1.5, (K, 1)) / s).astype(np.float32),
        "wb": (n((K, S)) / np.sqrt(K) / s).astype(np.float32),
        "tau2": np.random.uniform(0.3, 0.9, (C, 1)).astype(np.float32),
        "offs": striped(np.random.permutation(T)[:S]),
        "n1": striped8(np.stack([np.random.permutation(S) for _ in range(8)])),
        "n2": striped8(np.stack([np.random.permutation(S) for _ in range(8)])),
        "cand": striped(np.random.permutation(T)[:C]),
        "cb": striped(np.random.permutation(T)[:C]),
        "n3": striped8(np.stack([np.random.permutation(S) for _ in range(8)])),
        "n4": striped8(np.stack([np.random.permutation(S) for _ in range(8)])),
    }


def reference(x_words, x_scales, w1, tau, gs, wb, tau2, offs, n1, n2, cand, cb, n3, n4):
    x_cb = unpack_weight(x_words, x_scales)[:, unstriped(cb)]
    b = x_cb.T @ mxq(f64(wb), 0, "e4m3")
    top2 = b.max(axis=1, keepdims=True)
    ea2 = np.exp(f64(tau2) * (b[np.arange(C)[:, None], runs(n3, C)] - top2))
    x_cand = unpack_weight(x_words, x_scales)[:, unstriped(cand)]
    xq = unpack_weight(x_words, x_scales)[:, unstriped(offs)]
    y = mxq(f64(w1), 0, "e4m3").T @ xq
    top = y.max(axis=1, keepdims=True)
    ea = np.exp(f64(tau) * (y[np.arange(H)[:, None], runs(n2, H)] - top))
    z = f64(gs) * ((0.5 * (y - (y[np.arange(H)[:, None], runs(n1, H)]))) / (ea + 0.25))
    a = 0.0625 * ((x_cand.T @ mxq(z, 0, "e4m3")))
    return (2.0 * ea2) * (a - (a[np.arange(C)[:, None], runs(n4, C)])) - (0.5 * b)

@@ -1,0 +1,186 @@
+from contextlib import ExitStack
+
+import concourse.mybir as mybir
+
+K, T, S = 512, 2048, 512
+FLOPS = 3 * 2 * K * S * S
+
+F32 = mybir.dt.float32
+BF16 = mybir.dt.bfloat16
+I32 = mybir.dt.int32
+U32 = mybir.dt.uint32
+U16 = mybir.dt.uint16
+U8 = mybir.dt.uint8
+FP8X4 = mybir.dt.float8_e4m3fn_x4
+ALU = mybir.AluOpType
+ACT = mybir.ActivationFunctionType
+
+P = 128
+PACK = 4
+HALF = S // 2
+LINE = 4
+
+
+def tile_picked_cdswpxbera_none_p_kernel(tc, x_words, x_scales, w1, tau, gs, wb, tau2, offs, n1, n2, cand, cb, n3, n4, out):
+    nc = tc.nc
+    with ExitStack() as ctx:
+        keep = ctx.enter_context(tc.tile_pool(name="keep", bufs=1))
+        psum = ctx.enter_context(tc.psum_pool(name="psum", bufs=1))
+
+        def sb(name, shape, dtype, tag=None):
+            return keep.tile(shape, dtype, name=name, tag=tag or name, align_bytes=64)
+
+        def load_list(name, src):
+            t = sb(name, [P, S // 16], U16)
+            nc.sync.dma_start(t[:], src)
+            return t
+
+        def load_rows(name, src):
+            t = sb(name, [P, PACK], F32)
+            nc.gpsimd.dma_start(t[:], src.rearrange("(p t) o -> p (t o)", t=PACK))
+            return t
+
+        xw = sb("xw", [P, T], U32)
+        xs = sb("xs", [P, T], U8)
+        nc.vector.memset(xs[:].bitcast(I32), 0)
+        nc.sync.dma_start(xw[:].bitcast(I32), x_words[0].rearrange("p n t -> p (n t)").bitcast(I32))
+        l_offs = load_list("l_offs", offs)
+        for q in range(4):
+            nc.scalar.dma_start(xs[32 * q : 32 * q + 4, :].bitcast(I32), x_scales[0, 4 * q : 4 * q + 4, :].bitcast(I32))
+        w1_raw = [sb("w1_raw%d" % h, [P, PACK, HALF], F32) for h in range(2)]
+        for h in range(2):
+            nc.sync.dma_start(w1_raw[h][:], w1.rearrange("(p j) c -> p j c", j=PACK)[:, :, h * HALF : (h + 1) * HALF])
+        l_cand = load_list("l_cand", cand)
+        wb_raw = [sb("wb_raw%d" % h, [P, PACK, HALF], F32) for h in range(2)]
+        for h in range(2):
+            nc.sync.dma_start(wb_raw[h][:], wb.rearrange("(p j) c -> p j c", j=PACK)[:, :, h * HALF : (h + 1) * HALF])
+        l_n2 = load_list("l_n2", n2)
+        l_n1 = load_list("l_n1", n1)
+        l_cb = load_list("l_cb", cb)
+        l_n3 = load_list("l_n3", n3)
+        l_n4 = load_list("l_n4", n4)
+
+        tau_sb = load_rows("tau_sb", tau)
+        ywin = [sb("ywin%d" % t, [P, 2 * S], F32) for t in range(PACK)]
+        bwin = [sb("bwin%d" % t, [P, 2 * S], F32) for t in range(PACK)]
+        for w in ywin + bwin:
+            nc.gpsimd.memset(w[:, S:], 0.0)
+        gs_sb = load_rows("gs_sb", gs)
+        tau2_sb = load_rows("tau2_sb", tau2)
+
+        def pick(name, src, lst, dealt, tag=None):
+            dst = sb(name, [P, S], src.dtype, tag)
+            view = dst[:].rearrange("p (t m) -> p m t", t=PACK) if dealt else dst[:]
+            nc.vector.tensor_copy(view, src[:].indirect(lst[:]))
+            return dst
+
+        def quantize(name, grouped, width):
+            codes = sb(name + "_w", [P, width], U32)
+            scales = sb(name + "_s", [P, width], U8)
+            nc.vector.quantize_mx(out=codes[:].bitcast(FP8X4), scales=scales[:], in_=grouped)
+            return codes, scales
+
+        def product(dst, lhs, t, rhs):
+            cols = slice(t * P, (t + 1) * P)
+            nc.tensor.matmul_mx(out=dst, lhsT=lhs[0][:, cols].bitcast(FP8X4), lhsT_scale=lhs[1][:, cols],
+                                rhs=rhs[0][:].bitcast(FP8X4), rhs_scale=rhs[1][:], start=True, stop=True)
+
+        def copy_with_bias(win, bank, rate, top, bias):
+            nc.vector.tensor_scalar(win[:, :S], bank[:], 1.0, None, ALU.mult, ALU.max, accum_out=top)
+            nc.vector.tensor_scalar(bias, top, rate, -1.0, ALU.mult, ALU.mult)
+
+        xq = (pick("xq_w", xw, l_offs, False), pick("xq_s", xs, l_offs, False))
+
+        w1_bf = sb("w1_bf", [P, PACK, P, PACK], BF16)
+        for h in range(2):
+            m = slice(h * P // 2, (h + 1) * P // 2)
+            nc.scalar.activation(w1_bf[:, :, m, :].rearrange("p t m j -> p m t j"), w1_raw[h][:].rearrange("p j (m t) -> p m t j", t=PACK), ACT.Copy)
+        xcand_w = pick("xcand_w", xw, l_cand, True)
+        w1q = quantize("w1q", w1_bf[:].rearrange("p t m j -> p (t m j)"), S)
+        xcand = (xcand_w, pick("xcand_s", xs, l_cand, True, "w1_bf"))
+
+        wb_bf = sb("wb_bf", [P, S, PACK], BF16)
+        for h in range(2):
+            c = slice(h * HALF, (h + 1) * HALF)
+            nc.scalar.activation(wb_bf[:, c, :].rearrange("p (c i) j -> p c j i", i=LINE), wb_raw[h][:].rearrange("p j (c i) -> p c j i", i=LINE), ACT.Copy)
+
+        ybank = [psum.tile([P, S], F32, name="ybank%d" % t, tag="ya%d" % t) for t in range(PACK)]
+        top = sb("top", [P, PACK], F32)
+        nb = sb("nb", [P, PACK], F32)
+        ea = sb("ea", [P, PACK, S], F32)
+        for t in range(PACK):
+            product(ybank[t][:], w1q, t, xq)
+        for t in range(PACK):
+            copy_with_bias(ywin[t], ybank[t], tau_sb[:, t : t + 1], top[:, t : t + 1], nb[:, t : t + 1])
+            nc.scalar.activation(ea[:, t, :], ywin[t][:].indirect(l_n2[:]), ACT.Exp, bias=nb[:, t : t + 1], scale=tau_sb[:, t : t + 1])
+
+        g1 = sb("g1", [P, PACK, S], F32)
+        d = sb("d", [P, PACK, S], F32)
+        for t in range(2):
+            nc.vector.tensor_copy(g1[:, t, :], ywin[t][:].indirect(l_n1[:]))
+
+        s = sb("s", [P, PACK, S], F32)
+        for h in range(2):
+            c = slice(h * HALF, (h + 1) * HALF)
+            nc.scalar.activation(s[:, :, c], ea[:, :, c], ACT.Abs_reciprocal_sqrt, bias=0.5, scale=2.0)
+        for t in range(2, PACK):
+            nc.scalar.activation(g1[:, t, :], ywin[t][:].indirect(l_n1[:]), ACT.Copy)
+
+        xcb = (pick("xcb_w", xw, l_cb, True, "xq_w"), pick("xcb_s", xs, l_cb, True, "xq_s"))
+        wbq = quantize("wbq", wb_bf[:].rearrange("p c j -> p (c j)"), S)
+        bbank = [psum.tile([P, S], F32, name="bbank%d" % t) for t in range(PACK)]
+        top2 = sb("top2", [P, PACK], F32)
+        nb2 = sb("nb2", [P, PACK], F32)
+        ea2 = sb("ea2", [P, PACK, S], F32)
+        for t in range(PACK):
+            product(bbank[t][:], xcb, t, wbq)
+
+        def diff(t):
+            nc.vector.tensor_tensor(d[:, t, :], ybank[t][:], g1[:, t, :], ALU.subtract)
+
+        def b_side(t):
+            copy_with_bias(bwin[t], bbank[t], tau2_sb[:, t : t + 1], top2[:, t : t + 1], nb2[:, t : t + 1])
+            nc.scalar.activation(ea2[:, t, :], bwin[t][:].indirect(l_n3[:]), ACT.Exp, bias=nb2[:, t : t + 1], scale=tau2_sb[:, t : t + 1])
+
+        u = sb("u", [P, PACK, S], F32)
+
+        def weight(h):
+            c = slice(h * HALF, (h + 1) * HALF)
+            for t in range(PACK):
+                nc.vector.scalar_tensor_tensor(u[:, t, c], s[:, t, c], gs_sb[:, t : t + 1], s[:, t, c], ALU.mult, ALU.mult)
+
+        def score(h):
+            c = slice(h * HALF, (h + 1) * HALF)
+            z_bf = sb("z_bf%d" % h, [P, HALF, PACK], BF16)
+            nc.vector.tensor_tensor(z_bf[:].rearrange("p (c i) t -> p c t i", i=LINE), u[:, :, c].rearrange("p t (c i) -> p c t i", i=LINE),
+                                    d[:, :, c].rearrange("p t (c i) -> p c t i", i=LINE), ALU.mult)
+            zq = quantize("zq%d" % h, z_bf[:].rearrange("p c t -> p (c t)"), HALF)
+            for t in range(PACK):
+                product(abank[t][:, c], xcand, t, zq)
+
+        diff(0)
+        diff(1)
+        b_side(0)
+        b_side(1)
+        weight(0)
+        diff(2)
+        diff(3)
+        abank = [psum.tile([P, S], F32, name="abank%d" % t, tag="ya%d" % t) for t in range(PACK)]
+        score(0)
+        b_side(2)
+        b_side(3)
+        weight(1)
+        score(1)
+
+        out_rows = out.rearrange("(p t) n -> t p n", t=PACK)
+        for t in range(PACK):
+            nc.scalar.activation(ywin[t][:, :S], abank[t][:], ACT.Copy, scale=0.125)
+            g4 = sb("g4_%d" % t, [P, S], F32)
+            nc.scalar.activation(g4[:], ywin[t][:].indirect(l_n4[:]), ACT.Copy)
+            e = sb("e%d" % t, [P, S], F32)
+            nc.vector.scalar_tensor_tensor(e[:], abank[t][:], 0.125, g4[:], ALU.mult, ALU.subtract)
+            f = sb("f%d" % t, [P, S], F32)
+            nc.vector.tensor_tensor(f[:], e[:], ea2[:, t, :], ALU.mult)
+            res = sb("res%d" % t, [P, S], F32)
+            nc.vector.scalar_tensor_tensor(res[:], bbank[t][:], -0.5, f[:], ALU.mult, ALU.add)
+            nc.sync.dma_start(out_rows[t], res[:])

@@ -43,20 +43,23 @@ def tile_picked_cdswpxbera_none_p_kernel(tc, x_words, x_scales, w1, tau, gs, wb,
         xw = sb("xw", [P, T], U32)
         xs = sb("xs", [P, T], U8)
         nc.vector.memset(xs[:].bitcast(I32), 0)
-        nc.sync.dma_start(xw[:].bitcast(I32), x_words[0].rearrange("p n t -> p (n t)").bitcast(I32))
         l_offs = load_list("l_offs", offs)
+        nc.sync.dma_start(xw[:].bitcast(I32), x_words[0].rearrange("p n t -> p (n t)").bitcast(I32))
+        l_cand = load_list("l_cand", cand)
+        l_cb = load_list("l_cb", cb)
+        xs_in = sb("xs_in", [P, T], U8)
         for q in range(4):
-            nc.scalar.dma_start(xs[32 * q : 32 * q + 4, :].bitcast(I32), x_scales[0, 4 * q : 4 * q + 4, :].bitcast(I32))
+            nc.scalar.dma_start(xs_in[32 * q : 32 * q + 4, :].bitcast(I32), x_scales[0, 4 * q : 4 * q + 4, :].bitcast(I32))
+        for q in range(4):
+            nc.vector.tensor_copy(xs[32 * q : 32 * q + 4, :].bitcast(I32), xs_in[32 * q : 32 * q + 4, :].bitcast(I32))
         w1_raw = [sb("w1_raw%d" % h, [P, PACK, HALF], F32) for h in range(2)]
         for h in range(2):
             nc.sync.dma_start(w1_raw[h][:], w1.rearrange("(p j) c -> p j c", j=PACK)[:, :, h * HALF : (h + 1) * HALF])
-        l_cand = load_list("l_cand", cand)
+        l_n2 = load_list("l_n2", n2)
         wb_raw = [sb("wb_raw%d" % h, [P, PACK, HALF], F32) for h in range(2)]
         for h in range(2):
             nc.sync.dma_start(wb_raw[h][:], wb.rearrange("(p j) c -> p j c", j=PACK)[:, :, h * HALF : (h + 1) * HALF])
-        l_n2 = load_list("l_n2", n2)
         l_n1 = load_list("l_n1", n1)
-        l_cb = load_list("l_cb", cb)
         l_n3 = load_list("l_n3", n3)
         l_n4 = load_list("l_n4", n4)
 
@@ -87,17 +90,19 @@ def tile_picked_cdswpxbera_none_p_kernel(tc, x_words, x_scales, w1, tau, gs, wb,
 
         def copy_with_bias(win, bank, rate, top, bias):
             nc.vector.tensor_scalar(win[:, :S], bank[:], 1.0, None, ALU.mult, ALU.max, accum_out=top)
-            nc.vector.tensor_scalar(bias, top, rate, -1.0, ALU.mult, ALU.mult)
+            nc.gpsimd.tensor_scalar(bias, top, rate, -1.0, ALU.mult, ALU.mult)
 
-        xq = (pick("xq_w", xw, l_offs, False), pick("xq_s", xs, l_offs, False))
+        xq_s = pick("xq_s", xs, l_offs, False)
+        xq = (pick("xq_w", xw, l_offs, False), xq_s)
+        xcand_s = pick("xcand_s", xs, l_cand, True)
+        xcb_s = pick("xcb_s", xs, l_cb, True)
 
         w1_bf = sb("w1_bf", [P, PACK, P, PACK], BF16)
         for h in range(2):
             m = slice(h * P // 2, (h + 1) * P // 2)
             nc.scalar.activation(w1_bf[:, :, m, :].rearrange("p t m j -> p m t j"), w1_raw[h][:].rearrange("p j (m t) -> p m t j", t=PACK), ACT.Copy)
-        xcand_w = pick("xcand_w", xw, l_cand, True)
         w1q = quantize("w1q", w1_bf[:].rearrange("p t m j -> p (t m j)"), S)
-        xcand = (xcand_w, pick("xcand_s", xs, l_cand, True, "w1_bf"))
+        xcand = (pick("xcand_w", xw, l_cand, True, "w1_bf"), xcand_s)
 
         wb_bf = sb("wb_bf", [P, S, PACK], BF16)
         for h in range(2):
@@ -116,17 +121,14 @@ def tile_picked_cdswpxbera_none_p_kernel(tc, x_words, x_scales, w1, tau, gs, wb,
 
         g1 = sb("g1", [P, PACK, S], F32)
         d = sb("d", [P, PACK, S], F32)
-        for t in range(2):
-            nc.vector.tensor_copy(g1[:, t, :], ywin[t][:].indirect(l_n1[:]))
+        nc.scalar.activation(g1[:, 3, :], ywin[3][:].indirect(l_n1[:]), ACT.Copy)
 
         s = sb("s", [P, PACK, S], F32)
         for h in range(2):
             c = slice(h * HALF, (h + 1) * HALF)
             nc.scalar.activation(s[:, :, c], ea[:, :, c], ACT.Abs_reciprocal_sqrt, bias=0.5, scale=2.0)
-        for t in range(2, PACK):
-            nc.scalar.activation(g1[:, t, :], ywin[t][:].indirect(l_n1[:]), ACT.Copy)
-
-        xcb = (pick("xcb_w", xw, l_cb, True, "xq_w"), pick("xcb_s", xs, l_cb, True, "xq_s"))
+        nc.vector.tensor_copy(g1[:, 0, :], ywin[0][:].indirect(l_n1[:]))
+        xcb = (pick("xcb_w", xw, l_cb, True, "xq_w"), xcb_s)
         wbq = quantize("wbq", wb_bf[:].rearrange("p c j -> p (c j)"), S)
         bbank = [psum.tile([P, S], F32, name="bbank%d" % t) for t in range(PACK)]
         top2 = sb("top2", [P, PACK], F32)
@@ -134,9 +136,11 @@ def tile_picked_cdswpxbera_none_p_kernel(tc, x_words, x_scales, w1, tau, gs, wb,
         ea2 = sb("ea2", [P, PACK, S], F32)
         for t in range(PACK):
             product(bbank[t][:], xcb, t, wbq)
+        for t in (1, 2):
+            nc.vector.tensor_copy(g1[:, t, :], ywin[t][:].indirect(l_n1[:]))
 
         def diff(t):
-            nc.vector.tensor_tensor(d[:, t, :], ybank[t][:], g1[:, t, :], ALU.subtract)
+            nc.gpsimd.tensor_tensor(d[:, t, :], ywin[t][:, :S], g1[:, t, :], ALU.subtract)
 
         def b_side(t):
             copy_with_bias(bwin[t], bbank[t], tau2_sb[:, t : t + 1], top2[:, t : t + 1], nb2[:, t : t + 1])
@@ -158,17 +162,13 @@ def tile_picked_cdswpxbera_none_p_kernel(tc, x_words, x_scales, w1, tau, gs, wb,
             for t in range(PACK):
                 product(abank[t][:, c], xcand, t, zq)
 
-        diff(0)
-        diff(1)
-        b_side(0)
-        b_side(1)
+        for t in range(PACK):
+            diff(t)
+        for t in range(PACK):
+            b_side(t)
         weight(0)
-        diff(2)
-        diff(3)
         abank = [psum.tile([P, S], F32, name="abank%d" % t, tag="ya%d" % t) for t in range(PACK)]
         score(0)
-        b_side(2)
-        b_side(3)
         weight(1)
         score(1)
 
@@ -176,11 +176,14 @@ def tile_picked_cdswpxbera_none_p_kernel(tc, x_words, x_scales, w1, tau, gs, wb,
         for t in range(PACK):
             nc.scalar.activation(ywin[t][:, :S], abank[t][:], ACT.Copy, scale=0.125)
             g4 = sb("g4_%d" % t, [P, S], F32)
-            nc.scalar.activation(g4[:], ywin[t][:].indirect(l_n4[:]), ACT.Copy)
+            if t == 1:
+                nc.vector.tensor_copy(g4[:], ywin[t][:].indirect(l_n4[:]))
+            else:
+                nc.scalar.activation(g4[:], ywin[t][:].indirect(l_n4[:]), ACT.Copy)
             e = sb("e%d" % t, [P, S], F32)
             nc.vector.scalar_tensor_tensor(e[:], abank[t][:], 0.125, g4[:], ALU.mult, ALU.subtract)
             f = sb("f%d" % t, [P, S], F32)
-            nc.vector.tensor_tensor(f[:], e[:], ea2[:, t, :], ALU.mult)
+            (nc.vector if t == PACK - 1 else nc.gpsimd).tensor_tensor(f[:], e[:], ea2[:, t, :], ALU.mult)
             res = sb("res%d" % t, [P, S], F32)
             nc.vector.scalar_tensor_tensor(res[:], bbank[t][:], -0.5, f[:], ALU.mult, ALU.add)
             nc.sync.dma_start(out_rows[t], res[:])

@@ -35,41 +35,39 @@ def tile_picked_cdswpxbera_none_p_kernel(tc, x_words, x_scales, w1, tau, gs, wb,
             nc.sync.dma_start(t[:], src)
             return t
 
-        def load_rows(name, src):
+        def load_rows(name, src, queue):
             t = sb(name, [P, PACK], F32)
-            nc.gpsimd.dma_start(t[:], src.rearrange("(p t) o -> p (t o)", t=PACK))
+            queue.dma_start(t[:], src.rearrange("(p t) o -> p (t o)", t=PACK))
             return t
 
         xw = sb("xw", [P, T], U32)
         xs = sb("xs", [P, T], U8)
         nc.vector.memset(xs[:].bitcast(I32), 0)
         l_offs = load_list("l_offs", offs)
-        nc.sync.dma_start(xw[:].bitcast(I32), x_words[0].rearrange("p n t -> p (n t)").bitcast(I32))
+        w1_raw = [sb("w1_raw%d" % h, [P, PACK, HALF], F32) for h in range(2)]
+        for h in range(2):
+            nc.sync.dma_start(w1_raw[h][:], w1.rearrange("(p j) c -> p j c", j=PACK)[:, :, h * HALF : (h + 1) * HALF])
         l_cand = load_list("l_cand", cand)
-        l_cb = load_list("l_cb", cb)
         xs_in = sb("xs_in", [P, T], U8)
         for q in range(4):
             nc.scalar.dma_start(xs_in[32 * q : 32 * q + 4, :].bitcast(I32), x_scales[0, 4 * q : 4 * q + 4, :].bitcast(I32))
         for q in range(4):
             nc.vector.tensor_copy(xs[32 * q : 32 * q + 4, :].bitcast(I32), xs_in[32 * q : 32 * q + 4, :].bitcast(I32))
-        w1_raw = [sb("w1_raw%d" % h, [P, PACK, HALF], F32) for h in range(2)]
-        for h in range(2):
-            nc.sync.dma_start(w1_raw[h][:], w1.rearrange("(p j) c -> p j c", j=PACK)[:, :, h * HALF : (h + 1) * HALF])
+        nc.sync.dma_start(xw[:].bitcast(I32), x_words[0].rearrange("p n t -> p (n t)").bitcast(I32))
+        l_cb = load_list("l_cb", cb)
         l_n2 = load_list("l_n2", n2)
         wb_raw = [sb("wb_raw%d" % h, [P, PACK, HALF], F32) for h in range(2)]
         for h in range(2):
             nc.sync.dma_start(wb_raw[h][:], wb.rearrange("(p j) c -> p j c", j=PACK)[:, :, h * HALF : (h + 1) * HALF])
+        tau_sb = load_rows("tau_sb", tau, nc.gpsimd)
         l_n1 = load_list("l_n1", n1)
         l_n3 = load_list("l_n3", n3)
         l_n4 = load_list("l_n4", n4)
 
-        tau_sb = load_rows("tau_sb", tau)
         ywin = [sb("ywin%d" % t, [P, 2 * S], F32) for t in range(PACK)]
         bwin = [sb("bwin%d" % t, [P, 2 * S], F32) for t in range(PACK)]
-        for w in ywin + bwin:
-            nc.gpsimd.memset(w[:, S:], 0.0)
-        gs_sb = load_rows("gs_sb", gs)
-        tau2_sb = load_rows("tau2_sb", tau2)
+        gs_sb = load_rows("gs_sb", gs, nc.sync)
+        tau2_sb = load_rows("tau2_sb", tau2, nc.sync)
 
         def pick(name, src, lst, dealt, tag=None):
             dst = sb(name, [P, S], src.dtype, tag)
@@ -90,19 +88,18 @@ def tile_picked_cdswpxbera_none_p_kernel(tc, x_words, x_scales, w1, tau, gs, wb,
 
         def copy_with_bias(win, bank, rate, top, bias):
             nc.vector.tensor_scalar(win[:, :S], bank[:], 1.0, None, ALU.mult, ALU.max, accum_out=top)
-            nc.gpsimd.tensor_scalar(bias, top, rate, -1.0, ALU.mult, ALU.mult)
+            nc.vector.tensor_scalar(bias, top, rate, -1.0, ALU.mult, ALU.mult)
 
         xq_s = pick("xq_s", xs, l_offs, False)
-        xq = (pick("xq_w", xw, l_offs, False), xq_s)
         xcand_s = pick("xcand_s", xs, l_cand, True)
-        xcb_s = pick("xcb_s", xs, l_cb, True)
 
         w1_bf = sb("w1_bf", [P, PACK, P, PACK], BF16)
         for h in range(2):
             m = slice(h * P // 2, (h + 1) * P // 2)
             nc.scalar.activation(w1_bf[:, :, m, :].rearrange("p t m j -> p m t j"), w1_raw[h][:].rearrange("p j (m t) -> p m t j", t=PACK), ACT.Copy)
         w1q = quantize("w1q", w1_bf[:].rearrange("p t m j -> p (t m j)"), S)
-        xcand = (pick("xcand_w", xw, l_cand, True, "w1_bf"), xcand_s)
+        xq = (pick("xq_w", xw, l_offs, False), xq_s)
+        xcand = (pick("xcand_w", xw, l_cand, True), xcand_s)
 
         wb_bf = sb("wb_bf", [P, S, PACK], BF16)
         for h in range(2):
@@ -119,71 +116,71 @@ def tile_picked_cdswpxbera_none_p_kernel(tc, x_words, x_scales, w1, tau, gs, wb,
             copy_with_bias(ywin[t], ybank[t], tau_sb[:, t : t + 1], top[:, t : t + 1], nb[:, t : t + 1])
             nc.scalar.activation(ea[:, t, :], ywin[t][:].indirect(l_n2[:]), ACT.Exp, bias=nb[:, t : t + 1], scale=tau_sb[:, t : t + 1])
 
-        g1 = sb("g1", [P, PACK, S], F32)
-        d = sb("d", [P, PACK, S], F32)
-        nc.scalar.activation(g1[:, 3, :], ywin[3][:].indirect(l_n1[:]), ACT.Copy)
-
         s = sb("s", [P, PACK, S], F32)
-        for h in range(2):
-            c = slice(h * HALF, (h + 1) * HALF)
-            nc.scalar.activation(s[:, :, c], ea[:, :, c], ACT.Abs_reciprocal_sqrt, bias=0.5, scale=2.0)
-        nc.vector.tensor_copy(g1[:, 0, :], ywin[0][:].indirect(l_n1[:]))
-        xcb = (pick("xcb_w", xw, l_cb, True, "xq_w"), xcb_s)
+        nc.scalar.activation(s[:], ea[:], ACT.Abs_reciprocal_sqrt, bias=0.5, scale=2.0)
+        g0 = sb("g0", [P, S], F32)
+        g1 = [g0[:]] + [ea[:, t, :] for t in range(1, PACK)]
+        for t in range(1, PACK):
+            nc.scalar.activation(g1[t], ywin[t][:].indirect(l_n1[:]), ACT.Copy)
+
+        xcb = (pick("xcb_w", xw, l_cb, True, "xq_w"), pick("xcb_s", xs, l_cb, True, "xq_s"))
         wbq = quantize("wbq", wb_bf[:].rearrange("p c j -> p (c j)"), S)
         bbank = [psum.tile([P, S], F32, name="bbank%d" % t) for t in range(PACK)]
         top2 = sb("top2", [P, PACK], F32)
         nb2 = sb("nb2", [P, PACK], F32)
-        ea2 = sb("ea2", [P, PACK, S], F32)
         for t in range(PACK):
             product(bbank[t][:], xcb, t, wbq)
-        for t in (1, 2):
-            nc.vector.tensor_copy(g1[:, t, :], ywin[t][:].indirect(l_n1[:]))
 
-        def diff(t):
-            nc.gpsimd.tensor_tensor(d[:, t, :], ywin[t][:, :S], g1[:, t, :], ALU.subtract)
-
-        def b_side(t):
-            copy_with_bias(bwin[t], bbank[t], tau2_sb[:, t : t + 1], top2[:, t : t + 1], nb2[:, t : t + 1])
-            nc.scalar.activation(ea2[:, t, :], bwin[t][:].indirect(l_n3[:]), ACT.Exp, bias=nb2[:, t : t + 1], scale=tau2_sb[:, t : t + 1])
-
+        d = sb("d", [P, PACK, S], F32)
         u = sb("u", [P, PACK, S], F32)
 
-        def weight(h):
-            c = slice(h * HALF, (h + 1) * HALF)
-            for t in range(PACK):
-                nc.vector.scalar_tensor_tensor(u[:, t, c], s[:, t, c], gs_sb[:, t : t + 1], s[:, t, c], ALU.mult, ALU.mult)
+        def diff(t):
+            nc.vector.tensor_tensor(d[:, t, :], ybank[t][:], g1[t], ALU.subtract)
 
-        def score(h):
-            c = slice(h * HALF, (h + 1) * HALF)
-            z_bf = sb("z_bf%d" % h, [P, HALF, PACK], BF16)
-            nc.vector.tensor_tensor(z_bf[:].rearrange("p (c i) t -> p c t i", i=LINE), u[:, :, c].rearrange("p t (c i) -> p c t i", i=LINE),
-                                    d[:, :, c].rearrange("p t (c i) -> p c t i", i=LINE), ALU.mult)
-            zq = quantize("zq%d" % h, z_bf[:].rearrange("p c t -> p (c t)"), HALF)
-            for t in range(PACK):
-                product(abank[t][:, c], xcand, t, zq)
-
+        nc.vector.tensor_copy(g1[0], ywin[0][:].indirect(l_n1[:]))
         for t in range(PACK):
+            nc.vector.tensor_scalar(bwin[t][:, :S], bbank[t][:], 1.0, None, ALU.mult, ALU.max, accum_out=top2[:, t : t + 1])
+        diff(0)
+        nc.vector.scalar_tensor_tensor(nb2[:], top2[:], -1.0, tau2_sb[:], ALU.mult, ALU.mult)
+        for t in range(PACK):
+            nc.vector.scalar_tensor_tensor(u[:, t, :], s[:, t, :], gs_sb[:, t : t + 1], s[:, t, :], ALU.mult, ALU.mult)
+        for t in range(1, PACK):
             diff(t)
-        for t in range(PACK):
-            b_side(t)
-        weight(0)
+
         abank = [psum.tile([P, S], F32, name="abank%d" % t, tag="ya%d" % t) for t in range(PACK)]
-        score(0)
-        weight(1)
-        score(1)
+        halves = [slice(0, HALF), slice(HALF, S)]
+        z_bf = [sb("z_bf%d" % h, [P, HALF, PACK], BF16) for h in range(2)]
+        for h, c in enumerate(halves):
+            nc.vector.tensor_tensor(z_bf[h][:].rearrange("p (c i) t -> p c t i", i=LINE), u[:, :, c].rearrange("p t (c i) -> p c t i", i=LINE),
+                                    d[:, :, c].rearrange("p t (c i) -> p c t i", i=LINE), ALU.mult)
+        zq = [quantize("zq%d" % h, z_bf[h][:].rearrange("p c t -> p (c t)"), HALF) for h in range(2)]
+        for t in range(PACK):
+            for h, c in enumerate(halves):
+                product(abank[t][:, c], xcand, t, zq[h])
+
+        ea2 = s
+        for t in range(PACK):
+            nc.scalar.activation(ea2[:, t, :], bwin[t][:].indirect(l_n3[:]), ACT.Exp, bias=nb2[:, t : t + 1], scale=tau2_sb[:, t : t + 1])
 
         out_rows = out.rearrange("(p t) n -> t p n", t=PACK)
         for t in range(PACK):
-            nc.scalar.activation(ywin[t][:, :S], abank[t][:], ACT.Copy, scale=0.125)
             g4 = sb("g4_%d" % t, [P, S], F32)
-            if t == 1:
+            e = sb("e%d" % t, [P, S], F32)
+            f = sb("f%d" % t, [P, S], F32)
+            res = sb("res%d" % t, [P, S], F32)
+            if t == 0:
+                nc.vector.tensor_scalar(ywin[t][:, :S], abank[t][:], 0.125, None, ALU.mult)
                 nc.vector.tensor_copy(g4[:], ywin[t][:].indirect(l_n4[:]))
             else:
-                nc.scalar.activation(g4[:], ywin[t][:].indirect(l_n4[:]), ACT.Copy)
-            e = sb("e%d" % t, [P, S], F32)
-            nc.vector.scalar_tensor_tensor(e[:], abank[t][:], 0.125, g4[:], ALU.mult, ALU.subtract)
-            f = sb("f%d" % t, [P, S], F32)
-            (nc.vector if t == PACK - 1 else nc.gpsimd).tensor_tensor(f[:], e[:], ea2[:, t, :], ALU.mult)
-            res = sb("res%d" % t, [P, S], F32)
-            nc.vector.scalar_tensor_tensor(res[:], bbank[t][:], -0.5, f[:], ALU.mult, ALU.add)
-            nc.sync.dma_start(out_rows[t], res[:])
+                nc.scalar.activation(ywin[t][:, :S], abank[t][:], ACT.Copy, scale=0.125)
+            parts = [slice(0, HALF), slice(HALF, S)] if t == PACK - 1 else [slice(0, S)]
+            for c in parts:
+                if t > 0:
+                    nc.scalar.activation(g4[:, c], ywin[t][:].indirect(l_n4[:, c.start // 16 : c.stop // 16]), ACT.Copy)
+            for c in parts:
+                nc.vector.scalar_tensor_tensor(e[:, c], abank[t][:, c], 0.125, g4[:, c], ALU.mult, ALU.subtract)
+            for c in parts:
+                nc.vector.tensor_tensor(f[:, c], e[:, c], ea2[:, t, c], ALU.mult)
+            for c in parts:
+                nc.vector.scalar_tensor_tensor(res[:, c], bbank[t][:, c], -0.5, f[:, c], ALU.mult, ALU.add)
+                nc.sync.dma_start(out_rows[t][:, c], res[:, c])

@@ -43,18 +43,19 @@ def tile_picked_cdswpxbera_none_p_kernel(tc, x_words, x_scales, w1, tau, gs, wb,
         xw = sb("xw", [P, T], U32)
         xs = sb("xs", [P, T], U8)
         nc.vector.memset(xs[:].bitcast(I32), 0)
-        l_offs = load_list("l_offs", offs)
-        w1_raw = [sb("w1_raw%d" % h, [P, PACK, HALF], F32) for h in range(2)]
-        for h in range(2):
-            nc.sync.dma_start(w1_raw[h][:], w1.rearrange("(p j) c -> p j c", j=PACK)[:, :, h * HALF : (h + 1) * HALF])
-        l_cand = load_list("l_cand", cand)
         xs_in = sb("xs_in", [P, T], U8)
         for q in range(4):
-            nc.scalar.dma_start(xs_in[32 * q : 32 * q + 4, :].bitcast(I32), x_scales[0, 4 * q : 4 * q + 4, :].bitcast(I32))
+            nc.sync.dma_start(xs_in[32 * q : 32 * q + 4, :].bitcast(I32), x_scales[0, 4 * q : 4 * q + 4, :].bitcast(I32))
         for q in range(4):
             nc.vector.tensor_copy(xs[32 * q : 32 * q + 4, :].bitcast(I32), xs_in[32 * q : 32 * q + 4, :].bitcast(I32))
-        nc.sync.dma_start(xw[:].bitcast(I32), x_words[0].rearrange("p n t -> p (n t)").bitcast(I32))
+        l_offs = load_list("l_offs", offs)
+        w1_raw = [sb("w1_raw%d" % h, [P, PACK, HALF], F32) for h in range(2)]
+        w1_rows = w1.rearrange("(p j) c -> p j c", j=PACK)
+        nc.sync.dma_start(w1_raw[0][:], w1_rows[:, :, :HALF])
+        l_cand = load_list("l_cand", cand)
         l_cb = load_list("l_cb", cb)
+        nc.sync.dma_start(w1_raw[1][:], w1_rows[:, :, HALF:])
+        nc.sync.dma_start(xw[:].bitcast(I32), x_words[0].rearrange("p n t -> p (n t)").bitcast(I32))
         l_n2 = load_list("l_n2", n2)
         wb_raw = [sb("wb_raw%d" % h, [P, PACK, HALF], F32) for h in range(2)]
         for h in range(2):
@@ -92,6 +93,7 @@ def tile_picked_cdswpxbera_none_p_kernel(tc, x_words, x_scales, w1, tau, gs, wb,
 
         xq_s = pick("xq_s", xs, l_offs, False)
         xcand_s = pick("xcand_s", xs, l_cand, True)
+        xcb_s = pick("xcb_s", xs, l_cb, True)
 
         w1_bf = sb("w1_bf", [P, PACK, P, PACK], BF16)
         for h in range(2):
@@ -118,12 +120,12 @@ def tile_picked_cdswpxbera_none_p_kernel(tc, x_words, x_scales, w1, tau, gs, wb,
 
         s = sb("s", [P, PACK, S], F32)
         nc.scalar.activation(s[:], ea[:], ACT.Abs_reciprocal_sqrt, bias=0.5, scale=2.0)
-        g0 = sb("g0", [P, S], F32)
-        g1 = [g0[:]] + [ea[:, t, :] for t in range(1, PACK)]
-        for t in range(1, PACK):
+        g_first = sb("g_first", [P, 2, S], F32)
+        g1 = [g_first[:, 0, :], g_first[:, 1, :], ea[:, 2, :], ea[:, 3, :]]
+        for t in range(2, PACK):
             nc.scalar.activation(g1[t], ywin[t][:].indirect(l_n1[:]), ACT.Copy)
 
-        xcb = (pick("xcb_w", xw, l_cb, True, "xq_w"), pick("xcb_s", xs, l_cb, True, "xq_s"))
+        xcb = (pick("xcb_w", xw, l_cb, True, "xq_w"), xcb_s)
         wbq = quantize("wbq", wb_bf[:].rearrange("p c j -> p (c j)"), S)
         bbank = [psum.tile([P, S], F32, name="bbank%d" % t) for t in range(PACK)]
         top2 = sb("top2", [P, PACK], F32)
@@ -137,16 +139,17 @@ def tile_picked_cdswpxbera_none_p_kernel(tc, x_words, x_scales, w1, tau, gs, wb,
         def diff(t):
             nc.vector.tensor_tensor(d[:, t, :], ybank[t][:], g1[t], ALU.subtract)
 
-        nc.vector.tensor_copy(g1[0], ywin[0][:].indirect(l_n1[:]))
+        for t in range(2):
+            nc.vector.tensor_copy(g1[t], ywin[t][:].indirect(l_n1[:]))
         for t in range(PACK):
             nc.vector.tensor_scalar(bwin[t][:, :S], bbank[t][:], 1.0, None, ALU.mult, ALU.max, accum_out=top2[:, t : t + 1])
         diff(0)
+        diff(1)
         nc.vector.scalar_tensor_tensor(nb2[:], top2[:], -1.0, tau2_sb[:], ALU.mult, ALU.mult)
         for t in range(PACK):
             nc.vector.scalar_tensor_tensor(u[:, t, :], s[:, t, :], gs_sb[:, t : t + 1], s[:, t, :], ALU.mult, ALU.mult)
-        for t in range(1, PACK):
-            diff(t)
-
+        diff(2)
+        diff(3)
         abank = [psum.tile([P, S], F32, name="abank%d" % t, tag="ya%d" % t) for t in range(PACK)]
         halves = [slice(0, HALF), slice(HALF, S)]
         z_bf = [sb("z_bf%d" % h, [P, HALF, PACK], BF16) for h in range(2)]
@@ -158,29 +161,62 @@ def tile_picked_cdswpxbera_none_p_kernel(tc, x_words, x_scales, w1, tau, gs, wb,
             for h, c in enumerate(halves):
                 product(abank[t][:, c], xcand, t, zq[h])
 
-        ea2 = s
-        for t in range(PACK):
-            nc.scalar.activation(ea2[:, t, :], bwin[t][:].indirect(l_n3[:]), ACT.Exp, bias=nb2[:, t : t + 1], scale=tau2_sb[:, t : t + 1])
+        ea2 = [s[:, t, :] for t in range(PACK - 1)]
+
+        def b_fetch(t):
+            nc.scalar.activation(ea2[t], bwin[t][:].indirect(l_n3[:]), ACT.Exp, bias=nb2[:, t : t + 1], scale=tau2_sb[:, t : t + 1])
+
+        for t in range(PACK - 1):
+            b_fetch(t)
 
         out_rows = out.rearrange("(p t) n -> t p n", t=PACK)
-        for t in range(PACK):
-            g4 = sb("g4_%d" % t, [P, S], F32)
-            e = sb("e%d" % t, [P, S], F32)
-            f = sb("f%d" % t, [P, S], F32)
-            res = sb("res%d" % t, [P, S], F32)
+        g4 = [sb("g4_%d" % t, [P, S], F32) for t in range(PACK)]
+        e = [sb("e%d" % t, [P, S], F32) for t in range(PACK)]
+        f = [sb("f%d" % t, [P, S], F32) for t in range(PACK)]
+        res = [sb("res%d" % t, [P, S], F32) for t in range(PACK)]
+        whole = slice(0, S)
+
+        def a_copy(t):
             if t == 0:
                 nc.vector.tensor_scalar(ywin[t][:, :S], abank[t][:], 0.125, None, ALU.mult)
-                nc.vector.tensor_copy(g4[:], ywin[t][:].indirect(l_n4[:]))
             else:
                 nc.scalar.activation(ywin[t][:, :S], abank[t][:], ACT.Copy, scale=0.125)
-            parts = [slice(0, HALF), slice(HALF, S)] if t == PACK - 1 else [slice(0, S)]
-            for c in parts:
-                if t > 0:
-                    nc.scalar.activation(g4[:, c], ywin[t][:].indirect(l_n4[:, c.start // 16 : c.stop // 16]), ACT.Copy)
-            for c in parts:
-                nc.vector.scalar_tensor_tensor(e[:, c], abank[t][:, c], 0.125, g4[:, c], ALU.mult, ALU.subtract)
-            for c in parts:
-                nc.vector.tensor_tensor(f[:, c], e[:, c], ea2[:, t, c], ALU.mult)
-            for c in parts:
-                nc.vector.scalar_tensor_tensor(res[:, c], bbank[t][:, c], -0.5, f[:, c], ALU.mult, ALU.add)
-                nc.sync.dma_start(out_rows[t][:, c], res[:, c])
+
+        def a_fetch(t, c):
+            looked_up = ywin[t][:].indirect(l_n4[:, c.start // 16 : c.stop // 16])
+            if t == 0:
+                nc.vector.tensor_copy(g4[t][:, c], looked_up)
+            else:
+                nc.scalar.activation(g4[t][:, c], looked_up, ACT.Copy)
+
+        def step_e(t, c):
+            nc.vector.scalar_tensor_tensor(e[t][:, c], abank[t][:, c], 0.125, g4[t][:, c], ALU.mult, ALU.subtract)
+
+        def step_f(t, c):
+            nc.vector.tensor_tensor(f[t][:, c], e[t][:, c], ea2[t][:, c], ALU.mult)
+
+        def step_o(t, c):
+            nc.vector.scalar_tensor_tensor(res[t][:, c], bbank[t][:, c], -0.5, f[t][:, c], ALU.mult, ALU.add)
+            nc.sync.dma_start(out_rows[t][:, c], res[t][:, c])
+
+        a_copy(0)
+        a_copy(1)
+        a_fetch(0, whole)
+        a_fetch(1, whole)
+        a_copy(2)
+        a_fetch(2, whole)
+        step_e(0, whole)
+        step_e(1, whole)
+        ea2.append(sb("ea2_last", [P, S], F32, "g4_1")[:])
+        b_fetch(3)
+        a_copy(3)
+        step_f(0, whole)
+        step_f(1, whole)
+        step_o(0, whole)
+        step_e(2, whole)
+        step_o(1, whole)
+        step_f(2, whole)
+        step_o(2, whole)
+        for step in (a_fetch, step_e, step_f, step_o):
+            for c in halves:
+                step(3, c)

@@ -112,18 +112,18 @@ def tile_picked_cdswpxbera_none_p_kernel(tc, x_words, x_scales, w1, tau, gs, wb,
         top = sb("top", [P, PACK], F32)
         nb = sb("nb", [P, PACK], F32)
         ea = sb("ea", [P, PACK, S], F32)
+        y2 = [sb("y2_%d" % t, [P, S], F32) for t in range(PACK - 1)]
         for t in range(PACK):
             product(ybank[t][:], w1q, t, xq)
         for t in range(PACK):
             copy_with_bias(ywin[t], ybank[t], tau_sb[:, t : t + 1], top[:, t : t + 1], nb[:, t : t + 1])
             nc.scalar.activation(ea[:, t, :], ywin[t][:].indirect(l_n2[:]), ACT.Exp, bias=nb[:, t : t + 1], scale=tau_sb[:, t : t + 1])
+            if t < PACK - 1:
+                nc.sync.dma_start(y2[t][:], ywin[t][:, :S])
 
         s = sb("s", [P, PACK, S], F32)
         nc.scalar.activation(s[:], ea[:], ACT.Abs_reciprocal_sqrt, bias=0.5, scale=2.0)
-        g_first = sb("g_first", [P, 2, S], F32)
-        g1 = [g_first[:, 0, :], g_first[:, 1, :], ea[:, 2, :], ea[:, 3, :]]
-        for t in range(2, PACK):
-            nc.scalar.activation(g1[t], ywin[t][:].indirect(l_n1[:]), ACT.Copy)
+        nc.scalar.activation(ea[:, 3, :], ywin[3][:].indirect(l_n1[:]), ACT.Copy)
 
         xcb = (pick("xcb_w", xw, l_cb, True, "xq_w"), xcb_s)
         wbq = quantize("wbq", wb_bf[:].rearrange("p c j -> p (c j)"), S)
@@ -137,29 +137,38 @@ def tile_picked_cdswpxbera_none_p_kernel(tc, x_words, x_scales, w1, tau, gs, wb,
         u = sb("u", [P, PACK, S], F32)
 
         def diff(t):
-            nc.vector.tensor_tensor(d[:, t, :], ybank[t][:], g1[t], ALU.subtract)
+            nc.vector.tensor_tensor(d[:, t, :], ywin[t][:].indirect(l_n1[:]), y2[t][:], ALU.subtract)
 
-        for t in range(2):
-            nc.vector.tensor_copy(g1[t], ywin[t][:].indirect(l_n1[:]))
-        for t in range(PACK):
-            nc.vector.tensor_scalar(bwin[t][:, :S], bbank[t][:], 1.0, None, ALU.mult, ALU.max, accum_out=top2[:, t : t + 1])
+        def weight(t, c):
+            nc.vector.scalar_tensor_tensor(u[:, t, c], s[:, t, c], gs_sb[:, t : t + 1], s[:, t, c], ALU.mult, ALU.mult)
+
+        halves = [slice(0, HALF), slice(HALF, S)]
         diff(0)
         diff(1)
-        nc.vector.scalar_tensor_tensor(nb2[:], top2[:], -1.0, tau2_sb[:], ALU.mult, ALU.mult)
-        for t in range(PACK):
-            nc.vector.scalar_tensor_tensor(u[:, t, :], s[:, t, :], gs_sb[:, t : t + 1], s[:, t, :], ALU.mult, ALU.mult)
+        for t in range(PACK - 1):
+            nc.vector.tensor_scalar(bwin[t][:, :S], bbank[t][:], 1.0, None, ALU.mult, ALU.max, accum_out=top2[:, t : t + 1])
         diff(2)
-        diff(3)
+        nc.vector.scalar_tensor_tensor(nb2[:, :3], top2[:, :3], -1.0, tau2_sb[:, :3], ALU.mult, ALU.mult)
+        for t in range(PACK - 1):
+            weight(t, slice(0, S))
+        weight(3, halves[0])
+        nc.vector.tensor_tensor(d[:, 3, :], ea[:, 3, :], ybank[3][:], ALU.subtract)
+        weight(3, halves[1])
         abank = [psum.tile([P, S], F32, name="abank%d" % t, tag="ya%d" % t) for t in range(PACK)]
-        halves = [slice(0, HALF), slice(HALF, S)]
         z_bf = [sb("z_bf%d" % h, [P, HALF, PACK], BF16) for h in range(2)]
         for h, c in enumerate(halves):
             nc.vector.tensor_tensor(z_bf[h][:].rearrange("p (c i) t -> p c t i", i=LINE), u[:, :, c].rearrange("p t (c i) -> p c t i", i=LINE),
                                     d[:, :, c].rearrange("p t (c i) -> p c t i", i=LINE), ALU.mult)
-        zq = [quantize("zq%d" % h, z_bf[h][:].rearrange("p c t -> p (c t)"), HALF) for h in range(2)]
-        for t in range(PACK):
-            for h, c in enumerate(halves):
-                product(abank[t][:, c], xcand, t, zq[h])
+        zq = (sb("zq_w", [P, S], U32), sb("zq_s", [P, S], U8))
+        for h, c in enumerate(halves):
+            nc.vector.quantize_mx(out=zq[0][:, c].bitcast(FP8X4), scales=zq[1][:, c], in_=z_bf[h][:].rearrange("p c t -> p (c t)"))
+        for c in halves:
+            product(abank[0][:, c], xcand, 0, (zq[0][:, c], zq[1][:, c]))
+        for t in range(1, PACK):
+            product(abank[t][:], xcand, t, zq)
+
+        top_last = sb("top_last", [P, 1], F32, "z_bf0")
+        copy_with_bias(bwin[3], bbank[3], tau2_sb[:, 3:4], top_last[:], nb2[:, 3:4])
 
         ea2 = [s[:, t, :] for t in range(PACK - 1)]
 
@@ -178,9 +187,9 @@ def tile_picked_cdswpxbera_none_p_kernel(tc, x_words, x_scales, w1, tau, gs, wb,
 
         def a_copy(t):
             if t == 0:
-                nc.vector.tensor_scalar(ywin[t][:, :S], abank[t][:], 0.125, None, ALU.mult)
+                nc.vector.tensor_scalar(ywin[t][:, :S], abank[t][:], -0.125, None, ALU.mult)
             else:
-                nc.scalar.activation(ywin[t][:, :S], abank[t][:], ACT.Copy, scale=0.125)
+                nc.scalar.activation(ywin[t][:, :S], abank[t][:], ACT.Copy, scale=-0.125)
 
         def a_fetch(t, c):
             looked_up = ywin[t][:].indirect(l_n4[:, c.start // 16 : c.stop // 16])
@@ -190,7 +199,7 @@ def tile_picked_cdswpxbera_none_p_kernel(tc, x_words, x_scales, w1, tau, gs, wb,
                 nc.scalar.activation(g4[t][:, c], looked_up, ACT.Copy)
 
         def step_e(t, c):
-            nc.vector.scalar_tensor_tensor(e[t][:, c], abank[t][:, c], 0.125, g4[t][:, c], ALU.mult, ALU.subtract)
+            nc.vector.scalar_tensor_tensor(e[t][:, c], abank[t][:, c], -0.125, g4[t][:, c], ALU.mult, ALU.subtract)
 
         def step_f(t, c):
             nc.vector.tensor_tensor(f[t][:, c], e[t][:, c], ea2[t][:, c], ALU.mult)

from contextlib import ExitStack

import concourse.mybir as mybir

K, T, S = 512, 2048, 512
FLOPS = 3 * 2 * K * S * S

F32 = mybir.dt.float32
BF16 = mybir.dt.bfloat16
I32 = mybir.dt.int32
U32 = mybir.dt.uint32
U16 = mybir.dt.uint16
U8 = mybir.dt.uint8
FP8X4 = mybir.dt.float8_e4m3fn_x4
ALU = mybir.AluOpType
ACT = mybir.ActivationFunctionType

P = 128
PACK = 4
HALF = S // 2
LINE = 4


def tile_picked_cdswpxbera_none_p_kernel(tc, x_words, x_scales, w1, tau, gs, wb, tau2, offs, n1, n2, cand, cb, n3, n4, out):
    nc = tc.nc
    with ExitStack() as ctx:
        keep = ctx.enter_context(tc.tile_pool(name="keep", bufs=1))
        psum = ctx.enter_context(tc.psum_pool(name="psum", bufs=1))

        def sb(name, shape, dtype, tag=None):
            return keep.tile(shape, dtype, name=name, tag=tag or name, align_bytes=64)

        def load_list(name, src):
            t = sb(name, [P, S // 16], U16)
            nc.sync.dma_start(t[:], src)
            return t

        def load_rows(name, src, queue):
            t = sb(name, [P, PACK], F32)
            queue.dma_start(t[:], src.rearrange("(p t) o -> p (t o)", t=PACK))
            return t

        xw = sb("xw", [P, T], U32)
        xs = sb("xs", [P, T], U8)
        nc.vector.memset(xs[:].bitcast(I32), 0)
        xs_in = sb("xs_in", [P, T], U8)
        for q in range(4):
            nc.sync.dma_start(xs_in[32 * q : 32 * q + 4, :].bitcast(I32), x_scales[0, 4 * q : 4 * q + 4, :].bitcast(I32))
        for q in range(4):
            nc.vector.tensor_copy(xs[32 * q : 32 * q + 4, :].bitcast(I32), xs_in[32 * q : 32 * q + 4, :].bitcast(I32))
        l_offs = load_list("l_offs", offs)
        w1_raw = [sb("w1_raw%d" % h, [P, PACK, HALF], F32) for h in range(2)]
        w1_rows = w1.rearrange("(p j) c -> p j c", j=PACK)
        nc.sync.dma_start(w1_raw[0][:], w1_rows[:, :, :HALF])
        l_cand = load_list("l_cand", cand)
        l_cb = load_list("l_cb", cb)
        nc.sync.dma_start(w1_raw[1][:], w1_rows[:, :, HALF:])
        nc.sync.dma_start(xw[:].bitcast(I32), x_words[0].rearrange("p n t -> p (n t)").bitcast(I32))
        l_n2 = load_list("l_n2", n2)
        wb_raw = [sb("wb_raw%d" % h, [P, PACK, HALF], F32) for h in range(2)]
        for h in range(2):
            nc.sync.dma_start(wb_raw[h][:], wb.rearrange("(p j) c -> p j c", j=PACK)[:, :, h * HALF : (h + 1) * HALF])
        tau_sb = load_rows("tau_sb", tau, nc.gpsimd)
        l_n1 = load_list("l_n1", n1)
        l_n3 = load_list("l_n3", n3)
        l_n4 = load_list("l_n4", n4)

        ywin = [sb("ywin%d" % t, [P, 2 * S], F32) for t in range(PACK)]
        bwin = [sb("bwin%d" % t, [P, 2 * S], F32) for t in range(PACK)]
        gs_sb = load_rows("gs_sb", gs, nc.sync)
        tau2_sb = load_rows("tau2_sb", tau2, nc.sync)

        def pick(name, src, lst, dealt, tag=None):
            dst = sb(name, [P, S], src.dtype, tag)
            view = dst[:].rearrange("p (t m) -> p m t", t=PACK) if dealt else dst[:]
            nc.vector.tensor_copy(view, src[:].indirect(lst[:]))
            return dst

        def quantize(name, grouped, width):
            codes = sb(name + "_w", [P, width], U32)
            scales = sb(name + "_s", [P, width], U8)
            nc.vector.quantize_mx(out=codes[:].bitcast(FP8X4), scales=scales[:], in_=grouped)
            return codes, scales

        def product(dst, lhs, t, rhs):
            cols = slice(t * P, (t + 1) * P)
            nc.tensor.matmul_mx(out=dst, lhsT=lhs[0][:, cols].bitcast(FP8X4), lhsT_scale=lhs[1][:, cols],
                                rhs=rhs[0][:].bitcast(FP8X4), rhs_scale=rhs[1][:], start=True, stop=True)

        def copy_with_bias(win, bank, rate, top, bias):
            nc.vector.tensor_scalar(win[:, :S], bank[:], 1.0, None, ALU.mult, ALU.max, accum_out=top)
            nc.vector.tensor_scalar(bias, top, rate, -1.0, ALU.mult, ALU.mult)

        xq_s = pick("xq_s", xs, l_offs, False)
        xcand_s = pick("xcand_s", xs, l_cand, True)
        xcb_s = pick("xcb_s", xs, l_cb, True)

        w1_bf = sb("w1_bf", [P, PACK, P, PACK], BF16)
        for h in range(2):
            m = slice(h * P // 2, (h + 1) * P // 2)
            nc.scalar.activation(w1_bf[:, :, m, :].rearrange("p t m j -> p m t j"), w1_raw[h][:].rearrange("p j (m t) -> p m t j", t=PACK), ACT.Copy)
        w1q = quantize("w1q", w1_bf[:].rearrange("p t m j -> p (t m j)"), S)
        xq = (pick("xq_w", xw, l_offs, False), xq_s)
        xcand = (pick("xcand_w", xw, l_cand, True), xcand_s)

        wb_bf = sb("wb_bf", [P, S, PACK], BF16)
        for h in range(2):
            c = slice(h * HALF, (h + 1) * HALF)
            nc.scalar.activation(wb_bf[:, c, :].rearrange("p (c i) j -> p c j i", i=LINE), wb_raw[h][:].rearrange("p j (c i) -> p c j i", i=LINE), ACT.Copy)

        ybank = [psum.tile([P, S], F32, name="ybank%d" % t, tag="ya%d" % t) for t in range(PACK)]
        top = sb("top", [P, PACK], F32)
        nb = sb("nb", [P, PACK], F32)
        ea = sb("ea", [P, PACK, S], F32)
        y2 = [sb("y2_%d" % t, [P, S], F32) for t in range(PACK - 1)]
        for t in range(PACK):
            product(ybank[t][:], w1q, t, xq)
        for t in range(PACK):
            copy_with_bias(ywin[t], ybank[t], tau_sb[:, t : t + 1], top[:, t : t + 1], nb[:, t : t + 1])
            nc.scalar.activation(ea[:, t, :], ywin[t][:].indirect(l_n2[:]), ACT.Exp, bias=nb[:, t : t + 1], scale=tau_sb[:, t : t + 1])
            if t < PACK - 1:
                nc.sync.dma_start(y2[t][:], ywin[t][:, :S])

        s = sb("s", [P, PACK, S], F32)
        nc.scalar.activation(s[:], ea[:], ACT.Abs_reciprocal_sqrt, bias=0.5, scale=2.0)
        nc.scalar.activation(ea[:, 3, :], ywin[3][:].indirect(l_n1[:]), ACT.Copy)

        xcb = (pick("xcb_w", xw, l_cb, True, "xq_w"), xcb_s)
        wbq = quantize("wbq", wb_bf[:].rearrange("p c j -> p (c j)"), S)
        bbank = [psum.tile([P, S], F32, name="bbank%d" % t) for t in range(PACK)]
        top2 = sb("top2", [P, PACK], F32)
        nb2 = sb("nb2", [P, PACK], F32)
        for t in range(PACK):
            product(bbank[t][:], xcb, t, wbq)

        d = sb("d", [P, PACK, S], F32)
        u = sb("u", [P, PACK, S], F32)

        def diff(t):
            nc.vector.tensor_tensor(d[:, t, :], ywin[t][:].indirect(l_n1[:]), y2[t][:], ALU.subtract)

        def weight(t, c):
            nc.vector.scalar_tensor_tensor(u[:, t, c], s[:, t, c], gs_sb[:, t : t + 1], s[:, t, c], ALU.mult, ALU.mult)

        halves = [slice(0, HALF), slice(HALF, S)]
        diff(0)
        diff(1)
        for t in range(PACK - 1):
            nc.vector.tensor_scalar(bwin[t][:, :S], bbank[t][:], 1.0, None, ALU.mult, ALU.max, accum_out=top2[:, t : t + 1])
        diff(2)
        nc.vector.scalar_tensor_tensor(nb2[:, :3], top2[:, :3], -1.0, tau2_sb[:, :3], ALU.mult, ALU.mult)
        for t in range(PACK - 1):
            weight(t, slice(0, S))
        weight(3, halves[0])
        nc.vector.tensor_tensor(d[:, 3, :], ea[:, 3, :], ybank[3][:], ALU.subtract)
        weight(3, halves[1])
        abank = [psum.tile([P, S], F32, name="abank%d" % t, tag="ya%d" % t) for t in range(PACK)]
        z_bf = [sb("z_bf%d" % h, [P, HALF, PACK], BF16) for h in range(2)]
        for h, c in enumerate(halves):
            nc.vector.tensor_tensor(z_bf[h][:].rearrange("p (c i) t -> p c t i", i=LINE), u[:, :, c].rearrange("p t (c i) -> p c t i", i=LINE),
                                    d[:, :, c].rearrange("p t (c i) -> p c t i", i=LINE), ALU.mult)
        zq = (sb("zq_w", [P, S], U32), sb("zq_s", [P, S], U8))
        for h, c in enumerate(halves):
            nc.vector.quantize_mx(out=zq[0][:, c].bitcast(FP8X4), scales=zq[1][:, c], in_=z_bf[h][:].rearrange("p c t -> p (c t)"))
        for c in halves:
            product(abank[0][:, c], xcand, 0, (zq[0][:, c], zq[1][:, c]))
        for t in range(1, PACK):
            product(abank[t][:], xcand, t, zq)

        top_last = sb("top_last", [P, 1], F32, "z_bf0")
        copy_with_bias(bwin[3], bbank[3], tau2_sb[:, 3:4], top_last[:], nb2[:, 3:4])

        ea2 = [s[:, t, :] for t in range(PACK - 1)]

        def b_fetch(t):
            nc.scalar.activation(ea2[t], bwin[t][:].indirect(l_n3[:]), ACT.Exp, bias=nb2[:, t : t + 1], scale=tau2_sb[:, t : t + 1])

        for t in range(PACK - 1):
            b_fetch(t)

        out_rows = out.rearrange("(p t) n -> t p n", t=PACK)
        g4 = [sb("g4_%d" % t, [P, S], F32) for t in range(PACK)]
        e = [sb("e%d" % t, [P, S], F32) for t in range(PACK)]
        f = [sb("f%d" % t, [P, S], F32) for t in range(PACK)]
        res = [sb("res%d" % t, [P, S], F32) for t in range(PACK)]
        whole = slice(0, S)

        def a_copy(t):
            if t == 0:
                nc.vector.tensor_scalar(ywin[t][:, :S], abank[t][:], -0.125, None, ALU.mult)
            else:
                nc.scalar.activation(ywin[t][:, :S], abank[t][:], ACT.Copy, scale=-0.125)

        def a_fetch(t, c):
            looked_up = ywin[t][:].indirect(l_n4[:, c.start // 16 : c.stop // 16])
            if t == 0:
                nc.vector.tensor_copy(g4[t][:, c], looked_up)
            else:
                nc.scalar.activation(g4[t][:, c], looked_up, ACT.Copy)

        def step_e(t, c):
            nc.vector.scalar_tensor_tensor(e[t][:, c], abank[t][:, c], -0.125, g4[t][:, c], ALU.mult, ALU.subtract)

        def step_f(t, c):
            nc.vector.tensor_tensor(f[t][:, c], e[t][:, c], ea2[t][:, c], ALU.mult)

        def step_o(t, c):
            nc.vector.scalar_tensor_tensor(res[t][:, c], bbank[t][:, c], -0.5, f[t][:, c], ALU.mult, ALU.add)
            nc.sync.dma_start(out_rows[t][:, c], res[t][:, c])

        a_copy(0)
        a_copy(1)
        a_fetch(0, whole)
        a_fetch(1, whole)
        a_copy(2)
        a_fetch(2, whole)
        step_e(0, whole)
        step_e(1, whole)
        ea2.append(sb("ea2_last", [P, S], F32, "g4_1")[:])
        b_fetch(3)
        a_copy(3)
        step_f(0, whole)
        step_f(1, whole)
        step_o(0, whole)
        step_e(2, whole)
        step_o(1, whole)
        step_f(2, whole)
        step_o(2, whole)
        for step in (a_fetch, step_e, step_f, step_o):
            for c in halves:
                step(3, c)
